import numpy as np
import ml_dtypes


def mxq(x, axis, fmt="e4m3"):
    dtype, down = {"e4m3": (ml_dtypes.float8_e4m3fn, 7), "e5m2": (ml_dtypes.float8_e5m2, 14)}[fmt]
    v = np.moveaxis(np.asarray(x, np.float32).astype(ml_dtypes.bfloat16).astype(np.float64), axis, -1)
    blocks = v.reshape(v.shape[:-1] + (-1, 32))
    amax = np.abs(blocks).max(-1, keepdims=True)
    byte = np.maximum(np.where(amax > 0, np.frexp(amax)[1] - 1 + 127, 0) - down, 1)
    scale = np.exp2(byte - 127.0)
    codes = (blocks / scale).astype(np.float32).astype(dtype).astype(np.float64)
    return np.moveaxis((codes * scale).reshape(v.shape), -1, axis)


WIDE = False


def mx_kscale(k):
    if not WIDE:
        return np.ones(k)
    levels = np.array([18, -18])
    if k % 512:
        return np.exp2(np.random.permutation(np.resize(levels, k // 32))).repeat(32)
    a = np.empty((k // 512, 16))
    for p in range(k // 512):
        a[p, :8] = np.random.permutation(np.resize(levels, 8))
        for g in range(8):
            far = levels[np.abs(levels - a[p, g]) >= 10]
            a[p, g + 8] = far[np.random.randint(len(far))]
    return np.exp2(a.ravel()).repeat(32)


def f64(x):
    return np.asarray(x).astype(np.float64)


def striped(idx):
    return np.tile(np.asarray(idx).reshape(-1, 16).T, (8, 1)).astype(np.uint16)


def unstriped(offs):
    return offs[:16].T.reshape(-1).astype(np.int64)


B, N, T, D, DV = 1, 1024, 2048, 512, 512


def setup_inputs():
    n = np.random.standard_normal
    idx = np.random.permutation(T)[:B * N]
    u = np.ones(T)
    u[idx] = mx_kscale(B * N)
    coarse = lambda x: x.astype(np.float32).astype(ml_dtypes.bfloat16).astype(np.float64)
    r = np.random.randint(8, 33, T) / 16.0 * u
    return {
        "xT": (n((D, T)) / np.sqrt(N) / u).astype(np.float32),
        "dyT": (coarse(n((DV, T)))).astype(np.float32),
        "hT": (np.random.randint(1, 32, (DV, T)) / 32.0).astype(np.float32),
        "ts": np.tile(r, (128, 1)).astype(np.float32),
        "offs": striped(idx),
    }


def reference(xT, dyT, hT, ts, offs):
    idx = unstriped(offs)
    pick = lambda x: x[:, idx].reshape(x.shape[0], B, N).transpose(1, 0, 2)
    h = pick(f64(hT))
    dz = pick(f64(ts))[:, :1, :] * pick(f64(dyT)) * h * (1.0 - h)
    gw = mxq(pick(f64(xT)), 2, "e4m3") @ mxq(dz, 2, "e5m2").transpose(0, 2, 1)
    return gw

@@ -1,0 +1,303 @@
+from contextlib import ExitStack
+
+import concourse.mybir as mybir
+from concourse.masks import make_identity
+
+F32 = mybir.dt.float32
+BF16 = mybir.dt.bfloat16
+U32 = mybir.dt.uint32
+U16 = mybir.dt.uint16
+U8 = mybir.dt.uint8
+E4M3X4 = mybir.dt.float8_e4m3fn_x4
+E5M2X4 = mybir.dt.float8_e5m2_x4
+MULT = mybir.AluOpType.mult
+ADD = mybir.AluOpType.add
+SUB = mybir.AluOpType.subtract
+COPY = mybir.ActivationFunctionType.Copy
+IDENT = mybir.ActivationFunctionType.Identity
+
+P = 128
+SLOTS, TOKENS, D, DV = 1024, 2048, 512, 512
+PASS = 512
+PASSES = SLOTS // PASS
+BLOCKS = 4
+H0A = 1536
+FLOPS = 2 * SLOTS * D * DV
+
+
+def tile_attend_gex_sig_w_kernel(tc, xT, dyT, hT, ts, offs, out):
+    nc = tc.nc
+    with ExitStack() as ctx:
+        keep = ctx.enter_context(tc.tile_pool(name="keep", bufs=1))
+        psum = ctx.enter_context(tc.psum_pool(name="psum", bufs=1))
+        reuse = ctx.enter_context(tc.tile_pool(name="reuse", bufs=1))
+
+        offsets = keep.tile([P, SLOTS // 16], U16, name="offsets")
+        nc.sync.dma_start(offsets[:], offs)
+
+        ts_win = keep.tile([P, TOKENS], F32, name="ts_win")
+        nc.vector.memset(ts_win[:], 0.0)
+        win = {}
+        win["h", 0] = keep.tile([P, TOKENS], F32, name="win_h0")
+        nc.sync.dma_start(win["h", 0][:, :H0A], hT[0 * P : (0 + 1) * P, :H0A])
+        nc.sync.dma_start(ts_win[0:1, :], ts[0:1, :])
+        nc.sync.dma_start(win["h", 0][:, H0A:], hT[0 * P : (0 + 1) * P, H0A:])
+        win["x", 0] = keep.tile([P, TOKENS], F32, name="win_x0")
+        nc.sync.dma_start(win["x", 0][:, :], xT[0 * P : (0 + 1) * P, :])
+        win["dy", 0] = keep.tile([P, TOKENS], F32, name="win_dy0")
+        nc.sync.dma_start(win["dy", 0][:, :], dyT[0 * P : (0 + 1) * P, :])
+        win["h", 1] = reuse.tile([P, TOKENS], F32, name="win_h1", offset=0, align_bytes=64)
+        nc.sync.dma_start(win["h", 1][:, :], hT[1 * P : (1 + 1) * P, :])
+        win["x", 1] = keep.tile([P, TOKENS], F32, name="win_x1")
+        nc.sync.dma_start(win["x", 1][:, :], xT[1 * P : (1 + 1) * P, :])
+        win["dy", 1] = keep.tile([P, TOKENS], F32, name="win_dy1")
+        nc.sync.dma_start(win["dy", 1][:, :], dyT[1 * P : (1 + 1) * P, :])
+        win["h", 2] = reuse.tile([P, TOKENS], F32, name="win_h2", offset=8192, align_bytes=64)
+        nc.sync.dma_start(win["h", 2][:, :], hT[2 * P : (2 + 1) * P, :])
+        win["x", 2] = keep.tile([P, TOKENS], F32, name="win_x2")
+        nc.sync.dma_start(win["x", 2][:, :], xT[2 * P : (2 + 1) * P, :])
+        win["dy", 2] = keep.tile([P, TOKENS], F32, name="win_dy2")
+        nc.sync.dma_start(win["dy", 2][:, :], dyT[2 * P : (2 + 1) * P, :])
+        win["h", 3] = reuse.tile([P, TOKENS], F32, name="win_h3", offset=16384, align_bytes=64)
+        nc.sync.dma_start(win["h", 3][:, :], hT[3 * P : (3 + 1) * P, :])
+        win["x", 3] = reuse.tile([P, TOKENS], F32, name="win_x3", offset=49152, align_bytes=64)
+        nc.sync.dma_start(win["x", 3][:, :], xT[3 * P : (3 + 1) * P, :])
+        win["dy", 3] = keep.tile([P, TOKENS], F32, name="win_dy3")
+        nc.sync.dma_start(win["dy", 3][:, :], dyT[3 * P : (3 + 1) * P, :])
+
+        ident = keep.tile([P, P], F32, name="ident")
+        make_identity(nc, ident[:])
+
+        ts_row = keep.tile([P, SLOTS], F32, name="ts_row")
+        ts_col = keep.tile([P, SLOTS // P], F32, name="ts_col")
+        ts_neg = keep.tile([P, SLOTS // P], F32, name="ts_neg")
+        dz_codes = [keep.tile([P, DV], U32, name="dz_codes%d" % s, align_bytes=64) for s in range(PASSES)]
+        dz_scales = [keep.tile([P, DV], U8, name="dz_scales%d" % s, align_bytes=64) for s in range(PASSES)]
+        x_codes = [keep.tile([P, 2 * P], U32, name="x_codes%d" % k, align_bytes=64) for k in range(BLOCKS)]
+        x_scales = [keep.tile([P, 2 * P], U8, name="x_scales%d" % k, align_bytes=64) for k in range(BLOCKS)]
+        t = {}
+        bank = {("ts", 0): 2, ("ts", 1): 3, ("h", 0): 0, ("h", 1): 1, ("a", 0): 2, ("a", 1): 3, ("x", 0, None): 3, ("x", 1, None): 3, ("x", 2, None): 3, ("x", 3, 0): 0, ("x", 3, 1): 1, ("acc", 0): 4, ("acc", 1): 5, ("acc", 2): 6, ("acc", 3): 7}
+
+        def pc(s):
+            return slice(s * PASS, (s + 1) * PASS)
+
+        def TS():
+            nc.vector.tensor_copy(ts_row[:], ts_win[:].indirect(offsets[:]))
+            for s in range(PASSES):
+                turned = psum.tile([P, 4, P], F32, name="ts%d" % s, offset=2048 * bank["ts", s])
+                for c in range(4):
+                    nc.tensor.transpose(turned[:, c, :], plane(ts_row, s, c), ident[:])
+                nc.vector.tensor_copy(ts_col[:, 4 * s : 4 * s + 4], turned[:, :, 0])
+                nc.vector.tensor_scalar(ts_neg[:, 4 * s : 4 * s + 4], turned[:, :, 0], -1.0, None, MULT)
+
+        def plane(tile, s, c):
+            return tile[:, s * PASS + 2 * (c % 2) + c // 2 : (s + 1) * PASS : 4]
+
+        def Th(k, s):
+            turned = psum.tile([P, 4, P], F32, name="th%d%d" % (k, s), offset=2048 * bank["h", s])
+            for c in range(4):
+                nc.tensor.transpose(turned[:, c, :], plane(t["hg", k], s, c), ident[:])
+            t["Th", k, s] = turned
+
+        def Ta(k, s):
+            turned = psum.tile([P, 4, P], F32, name="ta%d%d" % (k, s), offset=2048 * bank["a", s])
+            for c in range(4):
+                nc.tensor.transpose(turned[:, c, :], plane(t["a", k], s, c), ident[:])
+            t["Ta", k, s] = turned
+
+        def Ut(k, s):
+            t["ut", k, s] = reuse.tile([P, 4, P], F32, name="ut%d%d" % (k, s), offset=(32768 + 4096 * k if k < 3 else 49152) + 2048 * s, align_bytes=64)
+            for c in range(4):
+                nc.scalar.activation(t["ut", k, s][:, c, :], t["Th", k, s][:, c, :], IDENT,
+                                     bias=ts_col[:, 4 * s + c : 4 * s + c + 1], scale=ts_neg[:, 4 * s + c : 4 * s + c + 1])
+
+        def G(k, s):
+            if s == 0:
+                t["gdz", k] = reuse.tile([P, 2 * PASS], BF16, name="gdz%d" % k, offset=8192 * k, align_bytes=64)
+            nc.vector.tensor_tensor(
+                t["gdz", k][:, pc(s)].rearrange("p (c i t) -> p c t i", i=4, t=4),
+                t["Ta", k, s][:].rearrange("p t (c i) -> p c t i", i=4),
+                t["ut", k, s][:].rearrange("p t (c i) -> p c t i", i=4),
+                MULT,
+            )
+
+        def H(k):
+            t["hg", k] = keep.tile([P, SLOTS], F32, name="hg%d" % k)
+            nc.vector.tensor_copy(t["hg", k][:], win["h", k][:].indirect(offsets[:]))
+
+        def Dy(k, s=None):
+            if s is None or s == 0:
+                t["a", k] = keep.tile([P, SLOTS], F32, name="a%d" % k)
+            if s is None:
+                nc.vector.tensor_tensor(t["a", k][:], win["dy", k][:].indirect(offsets[:]), t["hg", k][:], MULT)
+            else:
+                nc.vector.tensor_tensor(t["a", k][:, pc(s)], win["dy", k][:].indirect(offsets[:, 32 * s : 32 * (s + 1)]), t["hg", k][:, pc(s)], MULT)
+
+        def turn(name, k, s):
+            words = t[name, k][:].bitcast(F32)
+            turned = psum.tile([P, 4, P], F32, name="tx%d%s" % (k, s), offset=2048 * bank["x", k, s])
+            ss = range(PASSES) if s is None else [s]
+            for n, q in enumerate(ss):
+                for u in range(2):
+                    nc.tensor.transpose(turned[:, 2 * n + u, :], words[:, 256 * q + u : 256 * (q + 1) : 2], ident[:])
+            t["T" + name, k, s] = turned
+
+        def evac(name, k, s, eng):
+            turned = t["T" + name, k, s]
+            if s is None or s == 0:
+                t["g" + name, k] = keep.tile([P, 2 * PASS], BF16, name="gx%d" % k, align_bytes=64)
+            g = t["g" + name, k]
+            if s is None:
+                o = g[:].bitcast(F32).rearrange("p (q c u) -> p q c u", q=2, u=2)
+                i = turned[:].rearrange("p (q u) c -> p q c u", u=2)
+            else:
+                o = g[:, pc(s)].bitcast(F32).rearrange("p (c u) -> p c u", u=2)
+                i = turned[:, 0:2, :].rearrange("p u c -> p c u")
+            if eng == "s":
+                nc.scalar.copy(o, i)
+            else:
+                nc.vector.tensor_copy(o, i)
+
+        def Tx(k, s=None):
+            turn("xg", k, s)
+
+        def Ex(k, s=None):
+            evac("xg", k, s, "s")
+
+        def Qz(k, s):
+            cols = slice(k * P, (k + 1) * P)
+            nc.vector.quantize_mx(out=dz_codes[s][:, cols].bitcast(E5M2X4), scales=dz_scales[s][:, cols], in_=t["gdz", k][:, pc(s)])
+
+        def Qx(k, s=None):
+            cols = slice(0, 2 * P) if s is None else slice(s * P, (s + 1) * P)
+            src = t["gxg", k][:] if s is None else t["gxg", k][:, pc(s)]
+            nc.vector.quantize_mx(out=x_codes[k][:, cols].bitcast(E4M3X4), scales=x_scales[k][:, cols], in_=src)
+
+        def C(k, h=None):
+            if h is None or h == 0:
+                t["xb", k] = reuse.tile([P, TOKENS], BF16, name="x_bf%d" % k, offset=32768 + 4096 * k, align_bytes=64)
+            c = slice(0, TOKENS) if h is None else slice(h * 1024, (h + 1) * 1024)
+            nc.scalar.activation(t["xb", k][:, c], win["x", k][:, c], COPY)
+
+        def X(k, s=None):
+            if ("xg", k) not in t:
+                t["xg", k] = keep.tile([P, SLOTS], BF16, name="xg%d" % k)
+            c = slice(0, SLOTS) if s is None else pc(s)
+            o = offsets[:] if s is None else offsets[:, 32 * s : 32 * (s + 1)]
+            nc.scalar.activation(t["xg", k][:, c].rearrange("p (g b a) -> p g a b", a=2, b=2), t["xb", k][:].indirect(o), COPY)
+
+        def XV(k, s=None):
+            if ("xg", k) not in t:
+                t["xg", k] = keep.tile([P, SLOTS], BF16, name="xg%d" % k)
+            c = slice(0, SLOTS) if s is None else pc(s)
+            o = offsets[:] if s is None else offsets[:, 32 * s : 32 * (s + 1)]
+            nc.vector.tensor_copy(t["xg", k][:, c].rearrange("p (g b a) -> p g a b", a=2, b=2), win["x", k][:].indirect(o))
+
+        def M(j, s):
+            if s == 0:
+                t["acc", j] = psum.tile([P, DV], F32, name="acc%d" % j, offset=2048 * bank["acc", j])
+            cols = slice(s * P, (s + 1) * P)
+            nc.tensor.matmul_mx(
+                out=t["acc", j][:],
+                lhsT=x_codes[j][:, cols].bitcast(E4M3X4),
+                lhsT_scale=x_scales[j][:, cols],
+                rhs=dz_codes[s][:].bitcast(E5M2X4),
+                rhs_scale=dz_scales[s][:],
+                start=(s == 0),
+                stop=(s == PASSES - 1),
+            )
+
+        def O(j, v=0):
+            result = keep.tile([P, DV], F32, name="result%d" % j)
+            if v == 0:
+                nc.scalar.copy(result[:], t["acc", j][:])
+            else:
+                nc.vector.tensor_copy(result[:], t["acc", j][:])
+            nc.sync.dma_start(out[0, j * P : (j + 1) * P, :], result[:])
+
+        TS()
+        H(0)
+        Th(0, 0)
+        Th(0, 1)
+        C(0)
+        X(0)
+        Ut(0, 0)
+        Ut(0, 1)
+        Dy(0)
+        Ta(0, 0)
+        Ta(0, 1)
+        H(1)
+        Th(1, 0)
+        Th(1, 1)
+        G(0, 0)
+        G(0, 1)
+        Qz(0, 0)
+        Qz(0, 1)
+        Tx(0)
+        C(1)
+        Ex(0)
+        X(1)
+        Ut(1, 0)
+        Ut(1, 1)
+        Qx(0)
+        Dy(1)
+        Ta(1, 0)
+        Ta(1, 1)
+        H(2)
+        Th(2, 0)
+        Th(2, 1)
+        G(1, 0)
+        G(1, 1)
+        Qz(1, 0)
+        Qz(1, 1)
+        Tx(1)
+        C(2)
+        Ex(1)
+        X(2)
+        Ut(2, 0)
+        Ut(2, 1)
+        Qx(1)
+        Dy(2)
+        Ta(2, 0)
+        Ta(2, 1)
+        H(3)
+        Th(3, 0)
+        Th(3, 1)
+        G(2, 0)
+        G(2, 1)
+        Qz(2, 0)
+        Qz(2, 1)
+        Tx(2)
+        C(3)
+        Ex(2)
+        Ut(3, 0)
+        Ut(3, 1)
+        X(3, 0)
+        X(3, 1)
+        Qx(2)
+        Dy(3, 0)
+        Ta(3, 0)
+        Dy(3, 1)
+        Ta(3, 1)
+        Tx(3, 0)
+        Tx(3, 1)
+        Ex(3, 0)
+        Ex(3, 1)
+        G(3, 0)
+        G(3, 1)
+        Qz(3, 0)
+        Qz(3, 1)
+        Qx(3, 0)
+        Qx(3, 1)
+        M(0, 0)
+        M(1, 0)
+        M(2, 0)
+        M(0, 1)
+        O(0)
+        M(1, 1)
+        O(1, 1)
+        M(2, 1)
+        O(2)
+        M(3, 0)
+        M(3, 1)
+        O(3, 1)

@@ -11,8 +11,6 @@ U8 = mybir.dt.uint8
 E4M3X4 = mybir.dt.float8_e4m3fn_x4
 E5M2X4 = mybir.dt.float8_e5m2_x4
 MULT = mybir.AluOpType.mult
-ADD = mybir.AluOpType.add
-SUB = mybir.AluOpType.subtract
 COPY = mybir.ActivationFunctionType.Copy
 IDENT = mybir.ActivationFunctionType.Identity
 
@@ -21,7 +19,6 @@ SLOTS, TOKENS, D, DV = 1024, 2048, 512, 512
 PASS = 512
 PASSES = SLOTS // PASS
 BLOCKS = 4
-H0A = 1536
 FLOPS = 2 * SLOTS * D * DV
 
 
@@ -31,188 +28,195 @@ def tile_attend_gex_sig_w_kernel(tc, xT, dyT, hT, ts, offs, out):
         keep = ctx.enter_context(tc.tile_pool(name="keep", bufs=1))
         psum = ctx.enter_context(tc.psum_pool(name="psum", bufs=1))
         reuse = ctx.enter_context(tc.tile_pool(name="reuse", bufs=1))
+        place = {"x_bf0":0,"ut00":0,"ut01":2048,"x_bf1":4096,"ut10":4096,"ut11":6144,"x_bf2":8192,"ut20":8192,"ut21":10240,"win_x1":16384,"gx0":16384,"win_h1":40960,"gdz00":40960,"gdz01":41984,"win_x2":24576,"gx1":24576,"win_h2":49152,"gdz10":49152,"gdz11":50176,"win_x3":32768,"gx2":32768,"win_h3":57344,"gdz20":57344,"gdz21":58368,"ut30":34816,"ut31":36864,"win_dy0":65536,"ts_col":65536,"ts_neg":65600,"win_dy3":73728,"x_codes2":73728}
+        bank = {"ts0":2,"ts1":3,"th00":0,"th01":1,"ta00":2,"ta01":3,"tx0":0,"acc0":4,"th10":0,"th11":1,"ta10":2,"ta11":3,"tx1":0,"acc1":5,"th20":0,"th21":1,"ta20":2,"ta21":3,"tx2":0,"acc2":6,"th30":7,"th31":1,"ta30":2,"ta31":3,"tx3":0,"acc3":7,"tx30":0,"tx31":1}
+        t = {}
+
+        def put(name, shape, dtype):
+            if name not in t:
+                if name in place:
+                    t[name] = reuse.tile(shape, dtype, name=name, offset=place[name], align_bytes=64)
+                else:
+                    t[name] = keep.tile(shape, dtype, name=name, align_bytes=64)
+            return t[name]
+
+        def banked(name, shape):
+            if name not in t:
+                t[name] = psum.tile(shape, F32, name=name, offset=2048 * bank[name])
+            return t[name]
 
         offsets = keep.tile([P, SLOTS // 16], U16, name="offsets")
         nc.sync.dma_start(offsets[:], offs)
 
         ts_win = keep.tile([P, TOKENS], F32, name="ts_win")
         nc.vector.memset(ts_win[:], 0.0)
-        win = {}
-        win["h", 0] = keep.tile([P, TOKENS], F32, name="win_h0")
-        nc.sync.dma_start(win["h", 0][:, :H0A], hT[0 * P : (0 + 1) * P, :H0A])
+        source = {"h": hT, "dy": dyT, "x": xT}
+
+        def load(name, k, lo=0, hi=TOKENS):
+            win = put("win_%s%d" % (name, k), [P, TOKENS], F32)
+            nc.sync.dma_start(win[:, lo:hi], source[name][k * P : (k + 1) * P, lo:hi])
+
+        load("h", 0, 0, 1536)
         nc.sync.dma_start(ts_win[0:1, :], ts[0:1, :])
-        nc.sync.dma_start(win["h", 0][:, H0A:], hT[0 * P : (0 + 1) * P, H0A:])
-        win["x", 0] = keep.tile([P, TOKENS], F32, name="win_x0")
-        nc.sync.dma_start(win["x", 0][:, :], xT[0 * P : (0 + 1) * P, :])
-        win["dy", 0] = keep.tile([P, TOKENS], F32, name="win_dy0")
-        nc.sync.dma_start(win["dy", 0][:, :], dyT[0 * P : (0 + 1) * P, :])
-        win["h", 1] = reuse.tile([P, TOKENS], F32, name="win_h1", offset=0, align_bytes=64)
-        nc.sync.dma_start(win["h", 1][:, :], hT[1 * P : (1 + 1) * P, :])
-        win["x", 1] = keep.tile([P, TOKENS], F32, name="win_x1")
-        nc.sync.dma_start(win["x", 1][:, :], xT[1 * P : (1 + 1) * P, :])
-        win["dy", 1] = keep.tile([P, TOKENS], F32, name="win_dy1")
-        nc.sync.dma_start(win["dy", 1][:, :], dyT[1 * P : (1 + 1) * P, :])
-        win["h", 2] = reuse.tile([P, TOKENS], F32, name="win_h2", offset=8192, align_bytes=64)
-        nc.sync.dma_start(win["h", 2][:, :], hT[2 * P : (2 + 1) * P, :])
-        win["x", 2] = keep.tile([P, TOKENS], F32, name="win_x2")
-        nc.sync.dma_start(win["x", 2][:, :], xT[2 * P : (2 + 1) * P, :])
-        win["dy", 2] = keep.tile([P, TOKENS], F32, name="win_dy2")
-        nc.sync.dma_start(win["dy", 2][:, :], dyT[2 * P : (2 + 1) * P, :])
-        win["h", 3] = reuse.tile([P, TOKENS], F32, name="win_h3", offset=16384, align_bytes=64)
-        nc.sync.dma_start(win["h", 3][:, :], hT[3 * P : (3 + 1) * P, :])
-        win["x", 3] = reuse.tile([P, TOKENS], F32, name="win_x3", offset=49152, align_bytes=64)
-        nc.sync.dma_start(win["x", 3][:, :], xT[3 * P : (3 + 1) * P, :])
-        win["dy", 3] = keep.tile([P, TOKENS], F32, name="win_dy3")
-        nc.sync.dma_start(win["dy", 3][:, :], dyT[3 * P : (3 + 1) * P, :])
+        load("h", 0, 1536, 2048)
+        load("x", 0)
+        load("dy", 0)
+        load("h", 1)
+        load("x", 1)
+        load("dy", 1)
+        load("h", 2)
+        load("x", 2)
+        load("dy", 2)
+        load("h", 3)
+        load("x", 3)
+        load("dy", 3)
 
         ident = keep.tile([P, P], F32, name="ident")
         make_identity(nc, ident[:])
 
-        ts_row = keep.tile([P, SLOTS], F32, name="ts_row")
-        ts_col = keep.tile([P, SLOTS // P], F32, name="ts_col")
-        ts_neg = keep.tile([P, SLOTS // P], F32, name="ts_neg")
-        dz_codes = [keep.tile([P, DV], U32, name="dz_codes%d" % s, align_bytes=64) for s in range(PASSES)]
-        dz_scales = [keep.tile([P, DV], U8, name="dz_scales%d" % s, align_bytes=64) for s in range(PASSES)]
-        x_codes = [keep.tile([P, 2 * P], U32, name="x_codes%d" % k, align_bytes=64) for k in range(BLOCKS)]
-        x_scales = [keep.tile([P, 2 * P], U8, name="x_scales%d" % k, align_bytes=64) for k in range(BLOCKS)]
-        t = {}
-        bank = {("ts", 0): 2, ("ts", 1): 3, ("h", 0): 0, ("h", 1): 1, ("a", 0): 2, ("a", 1): 3, ("x", 0, None): 3, ("x", 1, None): 3, ("x", 2, None): 3, ("x", 3, 0): 0, ("x", 3, 1): 1, ("acc", 0): 4, ("acc", 1): 5, ("acc", 2): 6, ("acc", 3): 7}
+        dz_codes = [put("dz_codes%d" % s, [P, DV], U32) for s in range(PASSES)]
+        dz_scales = [put("dz_scales%d" % s, [P, DV], U8) for s in range(PASSES)]
 
         def pc(s):
-            return slice(s * PASS, (s + 1) * PASS)
+            return slice(0, SLOTS) if s is None else slice(s * PASS, (s + 1) * PASS)
 
-        def TS():
-            nc.vector.tensor_copy(ts_row[:], ts_win[:].indirect(offsets[:]))
-            for s in range(PASSES):
-                turned = psum.tile([P, 4, P], F32, name="ts%d" % s, offset=2048 * bank["ts", s])
-                for c in range(4):
-                    nc.tensor.transpose(turned[:, c, :], plane(ts_row, s, c), ident[:])
-                nc.vector.tensor_copy(ts_col[:, 4 * s : 4 * s + 4], turned[:, :, 0])
-                nc.vector.tensor_scalar(ts_neg[:, 4 * s : 4 * s + 4], turned[:, :, 0], -1.0, None, MULT)
+        def listed(s):
+            return offsets[:] if s is None else offsets[:, 32 * s : 32 * (s + 1)]
 
         def plane(tile, s, c):
-            return tile[:, s * PASS + 2 * (c % 2) + c // 2 : (s + 1) * PASS : 4]
+            return tile[:, s * PASS + c : (s + 1) * PASS : 4]
+
+        def planes(tile, s):
+            return tile[:, pc(s)]
+
+        def paired(k, s):
+            if s is None:
+                tile = put("xg%d" % k, [P, SLOTS], BF16)
+            else:
+                tile = put("xg%d%d" % (k, s), [P, PASS], BF16)
+            return tile[:].rearrange("p (u g e) -> p g u e", u=2, e=2)
+
+        def turn4(name, src, s):
+            turned = banked(name, [P, 4, P])
+            for c in range(4):
+                nc.tensor.transpose(turned[:, c, :], plane(src, s, c), ident[:])
+            return turned
+
+        def TS():
+            ts_row = put("ts_row", [P, SLOTS], F32)
+            nc.vector.tensor_copy(planes(ts_row, None), ts_win[:].indirect(offsets[:]))
+            for s in range(PASSES):
+                turn4("ts%d" % s, ts_row, s)
+
+        def TC():
+            for s in range(PASSES):
+                turned = t["ts%d" % s]
+                nc.vector.tensor_copy(put("ts_col", [P, 8], F32)[:, 4 * s : 4 * s + 4], turned[:, :, 0])
+                nc.vector.tensor_scalar(put("ts_neg", [P, 8], F32)[:, 4 * s : 4 * s + 4], turned[:, :, 0], -1.0, None, MULT)
+
+        def H(k, s=None):
+            nc.vector.tensor_copy(planes(put("hg%d" % k, [P, SLOTS], F32), s), t["win_h%d" % k][:].indirect(listed(s)))
+
+        def Dy(k, s=None):
+            nc.vector.tensor_tensor(planes(put("a%d" % k, [P, SLOTS], F32), s), t["win_dy%d" % k][:].indirect(listed(s)), planes(t["hg%d" % k], s), MULT)
 
         def Th(k, s):
-            turned = psum.tile([P, 4, P], F32, name="th%d%d" % (k, s), offset=2048 * bank["h", s])
-            for c in range(4):
-                nc.tensor.transpose(turned[:, c, :], plane(t["hg", k], s, c), ident[:])
-            t["Th", k, s] = turned
+            turn4("th%d%d" % (k, s), t["hg%d" % k], s)
 
         def Ta(k, s):
-            turned = psum.tile([P, 4, P], F32, name="ta%d%d" % (k, s), offset=2048 * bank["a", s])
-            for c in range(4):
-                nc.tensor.transpose(turned[:, c, :], plane(t["a", k], s, c), ident[:])
-            t["Ta", k, s] = turned
+            turn4("ta%d%d" % (k, s), t["a%d" % k], s)
 
         def Ut(k, s):
-            t["ut", k, s] = reuse.tile([P, 4, P], F32, name="ut%d%d" % (k, s), offset=(32768 + 4096 * k if k < 3 else 49152) + 2048 * s, align_bytes=64)
+            ut = put("ut%d%d" % (k, s), [P, 4, P], F32)
             for c in range(4):
-                nc.scalar.activation(t["ut", k, s][:, c, :], t["Th", k, s][:, c, :], IDENT,
-                                     bias=ts_col[:, 4 * s + c : 4 * s + c + 1], scale=ts_neg[:, 4 * s + c : 4 * s + c + 1])
+                col = slice(4 * s + c, 4 * s + c + 1)
+                nc.scalar.activation(ut[:, c, :], t["th%d%d" % (k, s)][:, c, :], IDENT, bias=t["ts_col"][:, col], scale=t["ts_neg"][:, col])
 
         def G(k, s):
-            if s == 0:
-                t["gdz", k] = reuse.tile([P, 2 * PASS], BF16, name="gdz%d" % k, offset=8192 * k, align_bytes=64)
+            gdz = put("gdz%d%d" % (k, s), [P, PASS], BF16)
             nc.vector.tensor_tensor(
-                t["gdz", k][:, pc(s)].rearrange("p (c i t) -> p c t i", i=4, t=4),
-                t["Ta", k, s][:].rearrange("p t (c i) -> p c t i", i=4),
-                t["ut", k, s][:].rearrange("p t (c i) -> p c t i", i=4),
+                gdz[:].rearrange("p (c i t) -> p c t i", i=4, t=4),
+                t["ta%d%d" % (k, s)][:].rearrange("p t (c i) -> p c t i", i=4),
+                t["ut%d%d" % (k, s)][:].rearrange("p t (c i) -> p c t i", i=4),
                 MULT,
             )
 
-        def H(k):
-            t["hg", k] = keep.tile([P, SLOTS], F32, name="hg%d" % k)
-            nc.vector.tensor_copy(t["hg", k][:], win["h", k][:].indirect(offsets[:]))
+        def Qz(k, s):
+            cols = slice(k * P, (k + 1) * P)
+            nc.vector.quantize_mx(out=dz_codes[s][:, cols].bitcast(E5M2X4), scales=dz_scales[s][:, cols], in_=t["gdz%d%d" % (k, s)][:])
 
-        def Dy(k, s=None):
-            if s is None or s == 0:
-                t["a", k] = keep.tile([P, SLOTS], F32, name="a%d" % k)
+        def C(k, h=None):
+            c = slice(0, TOKENS) if h is None else slice(h * 1024, (h + 1) * 1024)
+            nc.scalar.activation(put("x_bf%d" % k, [P, TOKENS], BF16)[:, c], t["win_x%d" % k][:, c], COPY)
+
+        def X(k, s=None):
+            nc.scalar.activation(paired(k, s), t["x_bf%d" % k][:].indirect(listed(s)), COPY)
+
+        def XV(k, s=None):
+            nc.vector.tensor_copy(paired(k, s), t["win_x%d" % k][:].indirect(listed(s)))
+
+        def Tx(k, s=None):
+            turned = banked("tx%d%s" % (k, "" if s is None else str(s)), [P, 4, P])
             if s is None:
-                nc.vector.tensor_tensor(t["a", k][:], win["dy", k][:].indirect(offsets[:]), t["hg", k][:], MULT)
+                words = t["xg%d" % k][:].bitcast(F32)
+                for q in range(PASSES):
+                    for u in range(2):
+                        nc.tensor.transpose(turned[:, 2 * q + u, :], words[:, 256 * u + P * q : 256 * u + P * (q + 1)], ident[:])
             else:
-                nc.vector.tensor_tensor(t["a", k][:, pc(s)], win["dy", k][:].indirect(offsets[:, 32 * s : 32 * (s + 1)]), t["hg", k][:, pc(s)], MULT)
-
-        def turn(name, k, s):
-            words = t[name, k][:].bitcast(F32)
-            turned = psum.tile([P, 4, P], F32, name="tx%d%s" % (k, s), offset=2048 * bank["x", k, s])
-            ss = range(PASSES) if s is None else [s]
-            for n, q in enumerate(ss):
+                words = t["xg%d%d" % (k, s)][:].bitcast(F32)
                 for u in range(2):
-                    nc.tensor.transpose(turned[:, 2 * n + u, :], words[:, 256 * q + u : 256 * (q + 1) : 2], ident[:])
-            t["T" + name, k, s] = turned
+                    nc.tensor.transpose(turned[:, u, :], words[:, P * u : P * (u + 1)], ident[:])
 
-        def evac(name, k, s, eng):
-            turned = t["T" + name, k, s]
-            if s is None or s == 0:
-                t["g" + name, k] = keep.tile([P, 2 * PASS], BF16, name="gx%d" % k, align_bytes=64)
-            g = t["g" + name, k]
+        def Ex(k, s=None, vec=False):
+            turned = t["tx%d%s" % (k, "" if s is None else str(s))]
+            g = put("gx%d" % k, [P, SLOTS], BF16)
             if s is None:
                 o = g[:].bitcast(F32).rearrange("p (q c u) -> p q c u", q=2, u=2)
                 i = turned[:].rearrange("p (q u) c -> p q c u", u=2)
             else:
                 o = g[:, pc(s)].bitcast(F32).rearrange("p (c u) -> p c u", u=2)
                 i = turned[:, 0:2, :].rearrange("p u c -> p c u")
-            if eng == "s":
-                nc.scalar.copy(o, i)
-            else:
+            if vec:
                 nc.vector.tensor_copy(o, i)
+            else:
+                nc.scalar.copy(o, i)
 
-        def Tx(k, s=None):
-            turn("xg", k, s)
-
-        def Ex(k, s=None):
-            evac("xg", k, s, "s")
-
-        def Qz(k, s):
-            cols = slice(k * P, (k + 1) * P)
-            nc.vector.quantize_mx(out=dz_codes[s][:, cols].bitcast(E5M2X4), scales=dz_scales[s][:, cols], in_=t["gdz", k][:, pc(s)])
+        def ExV(k, s=None):
+            Ex(k, s, True)
 
         def Qx(k, s=None):
             cols = slice(0, 2 * P) if s is None else slice(s * P, (s + 1) * P)
-            src = t["gxg", k][:] if s is None else t["gxg", k][:, pc(s)]
-            nc.vector.quantize_mx(out=x_codes[k][:, cols].bitcast(E4M3X4), scales=x_scales[k][:, cols], in_=src)
-
-        def C(k, h=None):
-            if h is None or h == 0:
-                t["xb", k] = reuse.tile([P, TOKENS], BF16, name="x_bf%d" % k, offset=32768 + 4096 * k, align_bytes=64)
-            c = slice(0, TOKENS) if h is None else slice(h * 1024, (h + 1) * 1024)
-            nc.scalar.activation(t["xb", k][:, c], win["x", k][:, c], COPY)
-
-        def X(k, s=None):
-            if ("xg", k) not in t:
-                t["xg", k] = keep.tile([P, SLOTS], BF16, name="xg%d" % k)
-            c = slice(0, SLOTS) if s is None else pc(s)
-            o = offsets[:] if s is None else offsets[:, 32 * s : 32 * (s + 1)]
-            nc.scalar.activation(t["xg", k][:, c].rearrange("p (g b a) -> p g a b", a=2, b=2), t["xb", k][:].indirect(o), COPY)
-
-        def XV(k, s=None):
-            if ("xg", k) not in t:
-                t["xg", k] = keep.tile([P, SLOTS], BF16, name="xg%d" % k)
-            c = slice(0, SLOTS) if s is None else pc(s)
-            o = offsets[:] if s is None else offsets[:, 32 * s : 32 * (s + 1)]
-            nc.vector.tensor_copy(t["xg", k][:, c].rearrange("p (g b a) -> p g a b", a=2, b=2), win["x", k][:].indirect(o))
+            codes = put("x_codes%d" % k, [P, 2 * P], U32)
+            scales = put("x_scales%d" % k, [P, 2 * P], U8)
+            nc.vector.quantize_mx(out=codes[:, cols].bitcast(E4M3X4), scales=scales[:, cols], in_=t["gx%d" % k][:, pc(s)])
 
         def M(j, s):
-            if s == 0:
-                t["acc", j] = psum.tile([P, DV], F32, name="acc%d" % j, offset=2048 * bank["acc", j])
             cols = slice(s * P, (s + 1) * P)
             nc.tensor.matmul_mx(
-                out=t["acc", j][:],
-                lhsT=x_codes[j][:, cols].bitcast(E4M3X4),
-                lhsT_scale=x_scales[j][:, cols],
+                out=banked("acc%d" % j, [P, DV])[:],
+                lhsT=t["x_codes%d" % j][:, cols].bitcast(E4M3X4),
+                lhsT_scale=t["x_scales%d" % j][:, cols],
                 rhs=dz_codes[s][:].bitcast(E5M2X4),
                 rhs_scale=dz_scales[s][:],
                 start=(s == 0),
                 stop=(s == PASSES - 1),
             )
 
+        def OH(j):
+            half = DV // 2
+            left = put("result%dl" % j, [P, half], F32)
+            right = put("result%dr" % j, [P, half], F32)
+            nc.scalar.copy(left[:], t["acc%d" % j][:, :half])
+            nc.sync.dma_start(out[0, j * P : (j + 1) * P, :half], left[:])
+            nc.vector.tensor_copy(right[:], t["acc%d" % j][:, half:])
+            nc.sync.dma_start(out[0, j * P : (j + 1) * P, half:], right[:])
+
         def O(j, v=0):
-            result = keep.tile([P, DV], F32, name="result%d" % j)
+            result = put("result%d" % j, [P, DV], F32)
             if v == 0:
-                nc.scalar.copy(result[:], t["acc", j][:])
+                nc.scalar.copy(result[:], t["acc%d" % j][:])
             else:
-                nc.vector.tensor_copy(result[:], t["acc", j][:])
+                nc.vector.tensor_copy(result[:], t["acc%d" % j][:])
             nc.sync.dma_start(out[0, j * P : (j + 1) * P, :], result[:])
 
         TS()
@@ -221,21 +225,22 @@ def tile_attend_gex_sig_w_kernel(tc, xT, dyT, hT, ts, offs, out):
         Th(0, 1)
         C(0)
         X(0)
+        Dy(0)
+        TC()
         Ut(0, 0)
         Ut(0, 1)
-        Dy(0)
         Ta(0, 0)
         Ta(0, 1)
+        Tx(0)
         H(1)
+        C(1)
+        Ex(0)
         Th(1, 0)
         Th(1, 1)
         G(0, 0)
         G(0, 1)
         Qz(0, 0)
         Qz(0, 1)
-        Tx(0)
-        C(1)
-        Ex(0)
         X(1)
         Ut(1, 0)
         Ut(1, 1)
@@ -243,16 +248,16 @@ def tile_attend_gex_sig_w_kernel(tc, xT, dyT, hT, ts, offs, out):
         Dy(1)
         Ta(1, 0)
         Ta(1, 1)
+        Tx(1)
         H(2)
+        C(2)
+        Ex(1)
         Th(2, 0)
         Th(2, 1)
         G(1, 0)
         G(1, 1)
         Qz(1, 0)
         Qz(1, 1)
-        Tx(1)
-        C(2)
-        Ex(1)
         X(2)
         Ut(2, 0)
         Ut(2, 1)
@@ -260,33 +265,33 @@ def tile_attend_gex_sig_w_kernel(tc, xT, dyT, hT, ts, offs, out):
         Dy(2)
         Ta(2, 0)
         Ta(2, 1)
+        Tx(2)
         H(3)
+        C(3)
+        Ex(2)
         Th(3, 0)
         Th(3, 1)
         G(2, 0)
         G(2, 1)
         Qz(2, 0)
         Qz(2, 1)
-        Tx(2)
-        C(3)
-        Ex(2)
         Ut(3, 0)
         Ut(3, 1)
         X(3, 0)
         X(3, 1)
-        Qx(2)
         Dy(3, 0)
         Ta(3, 0)
         Dy(3, 1)
         Ta(3, 1)
+        G(3, 0)
+        Qx(2)
+        Qz(3, 0)
+        G(3, 1)
+        Qz(3, 1)
         Tx(3, 0)
         Tx(3, 1)
         Ex(3, 0)
         Ex(3, 1)
-        G(3, 0)
-        G(3, 1)
-        Qz(3, 0)
-        Qz(3, 1)
         Qx(3, 0)
         Qx(3, 1)
         M(0, 0)

@@ -28,8 +28,8 @@ def tile_attend_gex_sig_w_kernel(tc, xT, dyT, hT, ts, offs, out):
         keep = ctx.enter_context(tc.tile_pool(name="keep", bufs=1))
         psum = ctx.enter_context(tc.psum_pool(name="psum", bufs=1))
         reuse = ctx.enter_context(tc.tile_pool(name="reuse", bufs=1))
-        place = {"x_bf0":0,"ut00":0,"ut01":2048,"x_bf1":4096,"ut10":4096,"ut11":6144,"x_bf2":8192,"ut20":8192,"ut21":10240,"win_x1":16384,"gx0":16384,"win_h1":40960,"gdz00":40960,"gdz01":41984,"win_x2":24576,"gx1":24576,"win_h2":49152,"gdz10":49152,"gdz11":50176,"win_x3":32768,"gx2":32768,"win_h3":57344,"gdz20":57344,"gdz21":58368,"ut30":34816,"ut31":36864,"win_dy0":65536,"ts_col":65536,"ts_neg":65600,"win_dy3":73728,"x_codes2":73728}
-        bank = {"ts0":2,"ts1":3,"th00":0,"th01":1,"ta00":2,"ta01":3,"tx0":0,"acc0":4,"th10":0,"th11":1,"ta10":2,"ta11":3,"tx1":0,"acc1":5,"th20":0,"th21":1,"ta20":2,"ta21":3,"tx2":0,"acc2":6,"th30":7,"th31":1,"ta30":2,"ta31":3,"tx3":0,"acc3":7,"tx30":0,"tx31":1}
+        place = {"x_bf0":83968,"ut00":84160,"ut01":86208,"x_bf1":90368,"ut10":90560,"ut11":92608,"x_bf2":96768,"ut20":96960,"ut21":99008,"x_bf3":103168,"ut30":103360,"ut31":105408,"win_x1":16384,"gx0":16384,"win_h1":40960,"gdz00":40960,"gdz01":41984,"win_x2":24576,"gx1":24576,"win_h2":49152,"gdz10":49152,"gdz11":50176,"win_x3":32768,"gx2":32768,"win_h3":57344,"gdz20":57344,"gdz21":58368,"ts_col":84032,"ts_neg":84096,"gdz31":73728,"x_codes2":73792,"x_codes3":72768}
+        bank = {"ts0":2,"ts1":3,"th00":0,"th01":1,"ta00":2,"ta01":3,"tx0":0,"acc0":5,"th10":0,"th11":1,"ta10":2,"ta11":3,"tx1":0,"acc1":6,"th20":0,"th21":1,"ta20":2,"ta21":3,"tx2":0,"acc2":0,"th30":7,"th31":1,"ta30":2,"ta31":3,"tx3":4,"acc3":7,"tx30":0,"tx31":1}
         t = {}
 
         def put(name, shape, dtype):
@@ -56,10 +56,10 @@ def tile_attend_gex_sig_w_kernel(tc, xT, dyT, hT, ts, offs, out):
             win = put("win_%s%d" % (name, k), [P, TOKENS], F32)
             nc.sync.dma_start(win[:, lo:hi], source[name][k * P : (k + 1) * P, lo:hi])
 
-        load("h", 0, 0, 1536)
+        load("x", 0, 0, 1536)
         nc.sync.dma_start(ts_win[0:1, :], ts[0:1, :])
-        load("h", 0, 1536, 2048)
-        load("x", 0)
+        load("x", 0, 1536, 2048)
+        load("h", 0)
         load("dy", 0)
         load("h", 1)
         load("x", 1)
@@ -111,8 +111,8 @@ def tile_attend_gex_sig_w_kernel(tc, xT, dyT, hT, ts, offs, out):
         def TC():
             for s in range(PASSES):
                 turned = t["ts%d" % s]
-                nc.vector.tensor_copy(put("ts_col", [P, 8], F32)[:, 4 * s : 4 * s + 4], turned[:, :, 0])
-                nc.vector.tensor_scalar(put("ts_neg", [P, 8], F32)[:, 4 * s : 4 * s + 4], turned[:, :, 0], -1.0, None, MULT)
+                nc.scalar.copy(put("ts_col", [P, 8], F32)[:, 4 * s : 4 * s + 4], turned[:, :, 0])
+                nc.scalar.activation(put("ts_neg", [P, 8], F32)[:, 4 * s : 4 * s + 4], turned[:, :, 0], COPY, scale=-1.0)
 
         def H(k, s=None):
             nc.vector.tensor_copy(planes(put("hg%d" % k, [P, SLOTS], F32), s), t["win_h%d" % k][:].indirect(listed(s)))
@@ -138,6 +138,19 @@ def tile_attend_gex_sig_w_kernel(tc, xT, dyT, hT, ts, offs, out):
                 gdz[:].rearrange("p (c i t) -> p c t i", i=4, t=4),
                 t["ta%d%d" % (k, s)][:].rearrange("p t (c i) -> p c t i", i=4),
                 t["ut%d%d" % (k, s)][:].rearrange("p t (c i) -> p c t i", i=4),
+                MULT,
+            )
+
+        def Ea(k, s):
+            at = put("at%d%d" % (k, s), [P, P, 4], F32)
+            nc.scalar.copy(at[:], t["ta%d%d" % (k, s)][:].rearrange("p t c -> p c t"))
+
+        def GG(k, s):
+            gdz = put("gdz%d%d" % (k, s), [P, PASS], BF16)
+            nc.gpsimd.tensor_tensor(
+                gdz[:].rearrange("p (c t) -> p c t", t=4),
+                t["at%d%d" % (k, s)][:],
+                t["ut%d%d" % (k, s)][:].rearrange("p t c -> p c t"),
                 MULT,
             )
 
@@ -219,16 +232,16 @@ def tile_attend_gex_sig_w_kernel(tc, xT, dyT, hT, ts, offs, out):
                 nc.vector.tensor_copy(result[:], t["acc%d" % j][:])
             nc.sync.dma_start(out[0, j * P : (j + 1) * P, :], result[:])
 
+        C(0)
+        X(0)
         TS()
         H(0)
         Th(0, 0)
         Th(0, 1)
-        C(0)
-        X(0)
-        Dy(0)
         TC()
         Ut(0, 0)
         Ut(0, 1)
+        Dy(0)
         Ta(0, 0)
         Ta(0, 1)
         Tx(0)
@@ -275,32 +288,28 @@ def tile_attend_gex_sig_w_kernel(tc, xT, dyT, hT, ts, offs, out):
         G(2, 1)
         Qz(2, 0)
         Qz(2, 1)
+        X(3)
         Ut(3, 0)
         Ut(3, 1)
-        X(3, 0)
-        X(3, 1)
         Dy(3, 0)
         Ta(3, 0)
         Dy(3, 1)
         Ta(3, 1)
+        Tx(3)
+        Ex(3)
         G(3, 0)
-        Qx(2)
         Qz(3, 0)
         G(3, 1)
         Qz(3, 1)
-        Tx(3, 0)
-        Tx(3, 1)
-        Ex(3, 0)
-        Ex(3, 1)
-        Qx(3, 0)
-        Qx(3, 1)
+        Qx(2)
+        Qx(3)
         M(0, 0)
-        M(1, 0)
-        M(2, 0)
         M(0, 1)
         O(0)
+        M(1, 0)
         M(1, 1)
         O(1, 1)
+        M(2, 0)
         M(2, 1)
         O(2)
         M(3, 0)

@@ -12,306 +12,269 @@ E4M3X4 = mybir.dt.float8_e4m3fn_x4
 E5M2X4 = mybir.dt.float8_e5m2_x4
 MULT = mybir.AluOpType.mult
 COPY = mybir.ActivationFunctionType.Copy
-IDENT = mybir.ActivationFunctionType.Identity
+IDENTITY = mybir.ActivationFunctionType.Identity
 
 P = 128
 SLOTS, TOKENS, D, DV = 1024, 2048, 512, 512
-PASS = 512
-PASSES = SLOTS // PASS
-BLOCKS = 4
+PACK = 4
+PASS = P * PACK
+BOTH = (0, 1)
+BLOCKS = D // P
+LAST = BLOCKS - 1
+LIST_COLUMNS = PASS // 16
 FLOPS = 2 * SLOTS * D * DV
+
+WINDOW_BYTES = TOKENS * 4
+HALF_KIB, KIB = 512, 1024
+X_WINDOWS = 0
+H_WINDOWS = X_WINDOWS + LAST * WINDOW_BYTES
+X_CASTS = H_WINDOWS + LAST * WINDOW_BYTES
+CAST_PITCH = TOKENS * 2 + 256
+TAIL = X_CASTS + LAST * CAST_PITCH
+
+
+def sbuf_places():
+    places = {}
+    for k in range(LAST):
+        places["x_win%d" % (k + 1)] = places["x_words%d" % k] = X_WINDOWS + k * WINDOW_BYTES
+        places["h_win%d" % (k + 1)] = H_WINDOWS + k * WINDOW_BYTES
+        places["x_cast%d" % k] = X_CASTS + k * CAST_PITCH
+        for s in BOTH:
+            places["dz%d%d" % (k, s)] = H_WINDOWS + k * WINDOW_BYTES + s * KIB
+            places["factor%d%d" % (k, s)] = X_CASTS + k * CAST_PITCH + 128 + s * 2 * KIB
+    places["ts_col"] = X_CASTS
+    places["ts_neg"] = X_CASTS + 64
+    for s in BOTH:
+        places["factor%d%d" % (LAST, s)] = places["x_win%d" % LAST] + (s + 1) * 2 * KIB
+    places["dz%d1" % LAST] = TAIL + HALF_KIB
+    places["x_codes%d" % (LAST - 1)] = TAIL
+    places["x_codes%d" % LAST] = TAIL + KIB
+    return places
+
+
+def psum_banks():
+    banks = {}
+    for s in BOTH:
+        banks["ts_turned%d" % s] = 2 + s
+        for k in range(BLOCKS):
+            banks["h_turned%d%d" % (k, s)] = s
+            banks["dyh_turned%d%d" % (k, s)] = 2 + s
+    for k in range(LAST):
+        banks["x_turned%d0" % k] = 0
+    banks["h_turned%d0" % LAST] = 7
+    banks["x_turned%d0" % LAST] = 4
+    banks["x_turned%d1" % LAST] = 0
+    for j, number in enumerate((5, 6, 1, 7)):
+        banks["acc%d" % j] = number
+    return banks
 
 
 def tile_attend_gex_sig_w_kernel(tc, xT, dyT, hT, ts, offs, out):
     nc = tc.nc
+    places, banks = sbuf_places(), psum_banks()
+    tiles = {}
+
     with ExitStack() as ctx:
         keep = ctx.enter_context(tc.tile_pool(name="keep", bufs=1))
         psum = ctx.enter_context(tc.psum_pool(name="psum", bufs=1))
-        reuse = ctx.enter_context(tc.tile_pool(name="reuse", bufs=1))
-        place = {"x_bf0":83968,"ut00":84160,"ut01":86208,"x_bf1":90368,"ut10":90560,"ut11":92608,"x_bf2":96768,"ut20":96960,"ut21":99008,"x_bf3":103168,"ut30":103360,"ut31":105408,"win_x1":16384,"gx0":16384,"win_h1":40960,"gdz00":40960,"gdz01":41984,"win_x2":24576,"gx1":24576,"win_h2":49152,"gdz10":49152,"gdz11":50176,"win_x3":32768,"gx2":32768,"win_h3":57344,"gdz20":57344,"gdz21":58368,"ts_col":84032,"ts_neg":84096,"gdz31":73728,"x_codes2":73792,"x_codes3":72768}
-        bank = {"ts0":2,"ts1":3,"th00":0,"th01":1,"ta00":2,"ta01":3,"tx0":0,"acc0":5,"th10":0,"th11":1,"ta10":2,"ta11":3,"tx1":0,"acc1":6,"th20":0,"th21":1,"ta20":2,"ta21":3,"tx2":0,"acc2":0,"th30":7,"th31":1,"ta30":2,"ta31":3,"tx3":4,"acc3":7,"tx30":0,"tx31":1}
-        t = {}
+        shared = ctx.enter_context(tc.tile_pool(name="shared", bufs=1))
 
-        def put(name, shape, dtype):
-            if name not in t:
-                if name in place:
-                    t[name] = reuse.tile(shape, dtype, name=name, offset=place[name], align_bytes=64)
+        def sbuf(name, shape, dtype):
+            if name not in tiles:
+                if name in places:
+                    tiles[name] = shared.tile(shape, dtype, name=name, offset=places[name], align_bytes=64)
                 else:
-                    t[name] = keep.tile(shape, dtype, name=name, align_bytes=64)
-            return t[name]
+                    tiles[name] = keep.tile(shape, dtype, name=name, align_bytes=64)
+            return tiles[name]
 
-        def banked(name, shape):
-            if name not in t:
-                t[name] = psum.tile(shape, F32, name=name, offset=2048 * bank[name])
-            return t[name]
+        def in_psum(name, shape):
+            if name not in tiles:
+                tiles[name] = psum.tile(shape, F32, name=name, offset=2 * KIB * banks[name])
+            return tiles[name]
+
+        def slots(passes):
+            return slice(passes[0] * PASS, (passes[-1] + 1) * PASS)
+
+        def block(k):
+            return slice(k * P, (k + 1) * P)
 
         offsets = keep.tile([P, SLOTS // 16], U16, name="offsets")
-        nc.sync.dma_start(offsets[:], offs)
+
+        def listed(window, passes):
+            return window[:].indirect(offsets[:, passes[0] * LIST_COLUMNS : (passes[-1] + 1) * LIST_COLUMNS])
 
         ts_win = keep.tile([P, TOKENS], F32, name="ts_win")
         nc.vector.memset(ts_win[:], 0.0)
-        source = {"h": hT, "dy": dyT, "x": xT}
 
-        def load(name, k, lo=0, hi=TOKENS):
-            win = put("win_%s%d" % (name, k), [P, TOKENS], F32)
-            nc.sync.dma_start(win[:, lo:hi], source[name][k * P : (k + 1) * P, lo:hi])
+        def load(name, source, k):
+            nc.sync.dma_start(sbuf("%s_win%d" % (name, k), [P, TOKENS], F32)[:], source[block(k), :])
 
-        load("x", 0, 0, 1536)
+        load("x", xT, 0)
+        nc.sync.dma_start(offsets[:], offs)
         nc.sync.dma_start(ts_win[0:1, :], ts[0:1, :])
-        load("x", 0, 1536, 2048)
-        load("h", 0)
-        load("dy", 0)
-        load("h", 1)
-        load("x", 1)
-        load("dy", 1)
-        load("h", 2)
-        load("x", 2)
-        load("dy", 2)
-        load("h", 3)
-        load("x", 3)
-        load("dy", 3)
+        load("h", hT, 0)
+        load("dy", dyT, 0)
+        for k in range(1, BLOCKS):
+            load("h", hT, k)
+            load("x", xT, k)
+            load("dy", dyT, k)
 
         ident = keep.tile([P, P], F32, name="ident")
         make_identity(nc, ident[:])
 
-        dz_codes = [put("dz_codes%d" % s, [P, DV], U32) for s in range(PASSES)]
-        dz_scales = [put("dz_scales%d" % s, [P, DV], U8) for s in range(PASSES)]
+        dz_codes = [sbuf("dz_codes%d" % s, [P, DV], U32) for s in BOTH]
+        dz_scales = [sbuf("dz_scales%d" % s, [P, DV], U8) for s in BOTH]
 
-        def pc(s):
-            return slice(0, SLOTS) if s is None else slice(s * PASS, (s + 1) * PASS)
+        def turn(name, gathered, s):
+            turned = in_psum(name, [P, PACK, P])
+            for t in range(PACK):
+                nc.tensor.transpose(turned[:, t, :], gathered[:, s * PASS + t : (s + 1) * PASS : PACK], ident[:])
 
-        def listed(s):
-            return offsets[:] if s is None else offsets[:, 32 * s : 32 * (s + 1)]
+        def gather_ts():
+            ts_row = sbuf("ts_row", [P, SLOTS], F32)
+            nc.vector.tensor_copy(ts_row[:], listed(ts_win, BOTH))
+            for s in BOTH:
+                turn("ts_turned%d" % s, ts_row, s)
 
-        def plane(tile, s, c):
-            return tile[:, s * PASS + c : (s + 1) * PASS : 4]
+        def copy_ts_columns():
+            for s in BOTH:
+                column = tiles["ts_turned%d" % s][:, :, 0]
+                of_pass = slice(PACK * s, PACK * (s + 1))
+                nc.scalar.copy(sbuf("ts_col", [P, 2 * PACK], F32)[:, of_pass], column)
+                nc.scalar.activation(sbuf("ts_neg", [P, 2 * PACK], F32)[:, of_pass], column, COPY, scale=-1.0)
 
-        def planes(tile, s):
-            return tile[:, pc(s)]
+        def gather_h(k):
+            nc.vector.tensor_copy(sbuf("h%d" % k, [P, SLOTS], F32)[:], listed(tiles["h_win%d" % k], BOTH))
 
-        def paired(k, s):
-            if s is None:
-                tile = put("xg%d" % k, [P, SLOTS], BF16)
-            else:
-                tile = put("xg%d%d" % (k, s), [P, PASS], BF16)
-            return tile[:].rearrange("p (u g e) -> p g u e", u=2, e=2)
+        def turn_h(k):
+            for s in BOTH:
+                turn("h_turned%d%d" % (k, s), tiles["h%d" % k], s)
 
-        def turn4(name, src, s):
-            turned = banked(name, [P, 4, P])
-            for c in range(4):
-                nc.tensor.transpose(turned[:, c, :], plane(src, s, c), ident[:])
-            return turned
+        def form_factor(k, s):
+            factor = sbuf("factor%d%d" % (k, s), [P, PACK, P], F32)
+            for t in range(PACK):
+                own = slice(PACK * s + t, PACK * s + t + 1)
+                nc.scalar.activation(
+                    factor[:, t, :],
+                    tiles["h_turned%d%d" % (k, s)][:, t, :],
+                    IDENTITY,
+                    bias=tiles["ts_col"][:, own],
+                    scale=tiles["ts_neg"][:, own],
+                )
 
-        def TS():
-            ts_row = put("ts_row", [P, SLOTS], F32)
-            nc.vector.tensor_copy(planes(ts_row, None), ts_win[:].indirect(offsets[:]))
-            for s in range(PASSES):
-                turn4("ts%d" % s, ts_row, s)
-
-        def TC():
-            for s in range(PASSES):
-                turned = t["ts%d" % s]
-                nc.scalar.copy(put("ts_col", [P, 8], F32)[:, 4 * s : 4 * s + 4], turned[:, :, 0])
-                nc.scalar.activation(put("ts_neg", [P, 8], F32)[:, 4 * s : 4 * s + 4], turned[:, :, 0], COPY, scale=-1.0)
-
-        def H(k, s=None):
-            nc.vector.tensor_copy(planes(put("hg%d" % k, [P, SLOTS], F32), s), t["win_h%d" % k][:].indirect(listed(s)))
-
-        def Dy(k, s=None):
-            nc.vector.tensor_tensor(planes(put("a%d" % k, [P, SLOTS], F32), s), t["win_dy%d" % k][:].indirect(listed(s)), planes(t["hg%d" % k], s), MULT)
-
-        def Th(k, s):
-            turn4("th%d%d" % (k, s), t["hg%d" % k], s)
-
-        def Ta(k, s):
-            turn4("ta%d%d" % (k, s), t["a%d" % k], s)
-
-        def Ut(k, s):
-            ut = put("ut%d%d" % (k, s), [P, 4, P], F32)
-            for c in range(4):
-                col = slice(4 * s + c, 4 * s + c + 1)
-                nc.scalar.activation(ut[:, c, :], t["th%d%d" % (k, s)][:, c, :], IDENT, bias=t["ts_col"][:, col], scale=t["ts_neg"][:, col])
-
-        def G(k, s):
-            gdz = put("gdz%d%d" % (k, s), [P, PASS], BF16)
+        def gather_dyh(k, passes):
+            dyh = sbuf("dyh%d" % k, [P, SLOTS], F32)
             nc.vector.tensor_tensor(
-                gdz[:].rearrange("p (c i t) -> p c t i", i=4, t=4),
-                t["ta%d%d" % (k, s)][:].rearrange("p t (c i) -> p c t i", i=4),
-                t["ut%d%d" % (k, s)][:].rearrange("p t (c i) -> p c t i", i=4),
+                dyh[:, slots(passes)], listed(tiles["dy_win%d" % k], passes), tiles["h%d" % k][:, slots(passes)], MULT
+            )
+            for s in passes:
+                turn("dyh_turned%d%d" % (k, s), dyh, s)
+
+        def form_dz(k, s):
+            nc.vector.tensor_tensor(
+                sbuf("dz%d%d" % (k, s), [P, PASS], BF16)[:].rearrange("p (c i t) -> p c t i", i=4, t=PACK),
+                tiles["dyh_turned%d%d" % (k, s)][:].rearrange("p t (c i) -> p c t i", i=4),
+                tiles["factor%d%d" % (k, s)][:].rearrange("p t (c i) -> p c t i", i=4),
                 MULT,
             )
 
-        def Ea(k, s):
-            at = put("at%d%d" % (k, s), [P, P, 4], F32)
-            nc.scalar.copy(at[:], t["ta%d%d" % (k, s)][:].rearrange("p t c -> p c t"))
-
-        def GG(k, s):
-            gdz = put("gdz%d%d" % (k, s), [P, PASS], BF16)
-            nc.gpsimd.tensor_tensor(
-                gdz[:].rearrange("p (c t) -> p c t", t=4),
-                t["at%d%d" % (k, s)][:],
-                t["ut%d%d" % (k, s)][:].rearrange("p t c -> p c t"),
-                MULT,
+        def quantise_dz(k, s):
+            nc.vector.quantize_mx(
+                out=dz_codes[s][:, block(k)].bitcast(E5M2X4),
+                scales=dz_scales[s][:, block(k)],
+                in_=tiles["dz%d%d" % (k, s)][:],
             )
 
-        def Qz(k, s):
-            cols = slice(k * P, (k + 1) * P)
-            nc.vector.quantize_mx(out=dz_codes[s][:, cols].bitcast(E5M2X4), scales=dz_scales[s][:, cols], in_=t["gdz%d%d" % (k, s)][:])
+        def cast_x(k):
+            nc.scalar.activation(sbuf("x_cast%d" % k, [P, TOKENS], BF16)[:], tiles["x_win%d" % k][:], COPY)
 
-        def C(k, h=None):
-            c = slice(0, TOKENS) if h is None else slice(h * 1024, (h + 1) * 1024)
-            nc.scalar.activation(put("x_bf%d" % k, [P, TOKENS], BF16)[:, c], t["win_x%d" % k][:, c], COPY)
+        def gather_x(k, passes):
+            pairs = sbuf("x_pairs%d%d" % (k, passes[0]), [P, len(passes) * PASS], BF16)
+            nc.scalar.activation(
+                pairs[:].rearrange("p (u g e) -> p g u e", u=2, e=2), listed(tiles["x_cast%d" % k], passes), COPY
+            )
 
-        def X(k, s=None):
-            nc.scalar.activation(paired(k, s), t["x_bf%d" % k][:].indirect(listed(s)), COPY)
-
-        def XV(k, s=None):
-            nc.vector.tensor_copy(paired(k, s), t["win_x%d" % k][:].indirect(listed(s)))
-
-        def Tx(k, s=None):
-            turned = banked("tx%d%s" % (k, "" if s is None else str(s)), [P, 4, P])
-            if s is None:
-                words = t["xg%d" % k][:].bitcast(F32)
-                for q in range(PASSES):
-                    for u in range(2):
-                        nc.tensor.transpose(turned[:, 2 * q + u, :], words[:, 256 * u + P * q : 256 * u + P * (q + 1)], ident[:])
-            else:
-                words = t["xg%d%d" % (k, s)][:].bitcast(F32)
+        def turn_x(k, passes):
+            words = tiles["x_pairs%d%d" % (k, passes[0])][:].bitcast(F32)
+            turned = in_psum("x_turned%d%d" % (k, passes[0]), [P, PACK, P])
+            for q in range(len(passes)):
                 for u in range(2):
-                    nc.tensor.transpose(turned[:, u, :], words[:, P * u : P * (u + 1)], ident[:])
+                    first = (u * len(passes) + q) * P
+                    nc.tensor.transpose(turned[:, 2 * q + u, :], words[:, first : first + P], ident[:])
 
-        def Ex(k, s=None, vec=False):
-            turned = t["tx%d%s" % (k, "" if s is None else str(s))]
-            g = put("gx%d" % k, [P, SLOTS], BF16)
-            if s is None:
-                o = g[:].bitcast(F32).rearrange("p (q c u) -> p q c u", q=2, u=2)
-                i = turned[:].rearrange("p (q u) c -> p q c u", u=2)
-            else:
-                o = g[:, pc(s)].bitcast(F32).rearrange("p (c u) -> p c u", u=2)
-                i = turned[:, 0:2, :].rearrange("p u c -> p c u")
-            if vec:
-                nc.vector.tensor_copy(o, i)
-            else:
-                nc.scalar.copy(o, i)
-
-        def ExV(k, s=None):
-            Ex(k, s, True)
-
-        def Qx(k, s=None):
-            cols = slice(0, 2 * P) if s is None else slice(s * P, (s + 1) * P)
-            codes = put("x_codes%d" % k, [P, 2 * P], U32)
-            scales = put("x_scales%d" % k, [P, 2 * P], U8)
-            nc.vector.quantize_mx(out=codes[:, cols].bitcast(E4M3X4), scales=scales[:, cols], in_=t["gx%d" % k][:, pc(s)])
-
-        def M(j, s):
-            cols = slice(s * P, (s + 1) * P)
-            nc.tensor.matmul_mx(
-                out=banked("acc%d" % j, [P, DV])[:],
-                lhsT=t["x_codes%d" % j][:, cols].bitcast(E4M3X4),
-                lhsT_scale=t["x_scales%d" % j][:, cols],
-                rhs=dz_codes[s][:].bitcast(E5M2X4),
-                rhs_scale=dz_scales[s][:],
-                start=(s == 0),
-                stop=(s == PASSES - 1),
+        def copy_x_words(k, passes):
+            x_words = sbuf("x_words%d" % k, [P, SLOTS], BF16)
+            turned = tiles["x_turned%d%d" % (k, passes[0])][:, 0 : 2 * len(passes), :]
+            nc.scalar.copy(
+                x_words[:, slots(passes)].bitcast(F32).rearrange("p (q d u) -> p q d u", d=P, u=2),
+                turned.rearrange("p (q u) d -> p q d u", u=2),
             )
 
-        def OH(j):
-            half = DV // 2
-            left = put("result%dl" % j, [P, half], F32)
-            right = put("result%dr" % j, [P, half], F32)
-            nc.scalar.copy(left[:], t["acc%d" % j][:, :half])
-            nc.sync.dma_start(out[0, j * P : (j + 1) * P, :half], left[:])
-            nc.vector.tensor_copy(right[:], t["acc%d" % j][:, half:])
-            nc.sync.dma_start(out[0, j * P : (j + 1) * P, half:], right[:])
+        def quantise_x(k):
+            nc.vector.quantize_mx(
+                out=sbuf("x_codes%d" % k, [P, 2 * P], U32)[:].bitcast(E4M3X4),
+                scales=sbuf("x_scales%d" % k, [P, 2 * P], U8)[:],
+                in_=tiles["x_words%d" % k][:],
+            )
 
-        def O(j, v=0):
-            result = put("result%d" % j, [P, DV], F32)
-            if v == 0:
-                nc.scalar.copy(result[:], t["acc%d" % j][:])
+        def multiply_and_store(j):
+            acc = in_psum("acc%d" % j, [P, DV])
+            for s in BOTH:
+                nc.tensor.matmul_mx(
+                    out=acc[:],
+                    lhsT=tiles["x_codes%d" % j][:, block(s)].bitcast(E4M3X4),
+                    lhsT_scale=tiles["x_scales%d" % j][:, block(s)],
+                    rhs=dz_codes[s][:].bitcast(E5M2X4),
+                    rhs_scale=dz_scales[s][:],
+                    start=(s == BOTH[0]),
+                    stop=(s == BOTH[-1]),
+                )
+            result = sbuf("result%d" % j, [P, DV], F32)
+            if j % 2 == 0:
+                nc.scalar.copy(result[:], acc[:])
             else:
-                nc.vector.tensor_copy(result[:], t["acc%d" % j][:])
-            nc.sync.dma_start(out[0, j * P : (j + 1) * P, :], result[:])
+                nc.vector.tensor_copy(result[:], acc[:])
+            nc.sync.dma_start(out[0, block(j), :], result[:])
 
-        C(0)
-        X(0)
-        TS()
-        H(0)
-        Th(0, 0)
-        Th(0, 1)
-        TC()
-        Ut(0, 0)
-        Ut(0, 1)
-        Dy(0)
-        Ta(0, 0)
-        Ta(0, 1)
-        Tx(0)
-        H(1)
-        C(1)
-        Ex(0)
-        Th(1, 0)
-        Th(1, 1)
-        G(0, 0)
-        G(0, 1)
-        Qz(0, 0)
-        Qz(0, 1)
-        X(1)
-        Ut(1, 0)
-        Ut(1, 1)
-        Qx(0)
-        Dy(1)
-        Ta(1, 0)
-        Ta(1, 1)
-        Tx(1)
-        H(2)
-        C(2)
-        Ex(1)
-        Th(2, 0)
-        Th(2, 1)
-        G(1, 0)
-        G(1, 1)
-        Qz(1, 0)
-        Qz(1, 1)
-        X(2)
-        Ut(2, 0)
-        Ut(2, 1)
-        Qx(1)
-        Dy(2)
-        Ta(2, 0)
-        Ta(2, 1)
-        Tx(2)
-        H(3)
-        C(3)
-        Ex(2)
-        Th(3, 0)
-        Th(3, 1)
-        G(2, 0)
-        G(2, 1)
-        Qz(2, 0)
-        Qz(2, 1)
-        X(3)
-        Ut(3, 0)
-        Ut(3, 1)
-        Dy(3, 0)
-        Ta(3, 0)
-        Dy(3, 1)
-        Ta(3, 1)
-        Tx(3)
-        Ex(3)
-        G(3, 0)
-        Qz(3, 0)
-        G(3, 1)
-        Qz(3, 1)
-        Qx(2)
-        Qx(3)
-        M(0, 0)
-        M(0, 1)
-        O(0)
-        M(1, 0)
-        M(1, 1)
-        O(1, 1)
-        M(2, 0)
-        M(2, 1)
-        O(2)
-        M(3, 0)
-        M(3, 1)
-        O(3, 1)
+        cast_x(0)
+        gather_x(0, BOTH)
+        gather_ts()
+        gather_h(0)
+        turn_h(0)
+        copy_ts_columns()
+        for s in BOTH:
+            form_factor(0, s)
+
+        for k in range(LAST):
+            gather_dyh(k, BOTH)
+            turn_x(k, BOTH)
+            gather_h(k + 1)
+            cast_x(k + 1)
+            copy_x_words(k, BOTH)
+            turn_h(k + 1)
+            for s in BOTH:
+                form_dz(k, s)
+            for s in BOTH:
+                quantise_dz(k, s)
+            if k + 1 < LAST:
+                gather_x(k + 1, BOTH)
+                for s in BOTH:
+                    form_factor(k + 1, s)
+                quantise_x(k)
+
+        for s in BOTH:
+            form_factor(LAST, s)
+            gather_x(LAST, (s,))
+        for s in BOTH:
+            gather_dyh(LAST, (s,))
+        for s in BOTH:
+            turn_x(LAST, (s,))
+        for s in BOTH:
+            copy_x_words(LAST, (s,))
+        for s in BOTH:
+            form_dz(LAST, s)
+            quantise_dz(LAST, s)
+        quantise_x(LAST - 1)
+        quantise_x(LAST)
+        for j in range(BLOCKS):
+            multiply_and_store(j)

from contextlib import ExitStack

import concourse.mybir as mybir
from concourse.masks import make_identity

F32 = mybir.dt.float32
BF16 = mybir.dt.bfloat16
U32 = mybir.dt.uint32
U16 = mybir.dt.uint16
U8 = mybir.dt.uint8
E4M3X4 = mybir.dt.float8_e4m3fn_x4
E5M2X4 = mybir.dt.float8_e5m2_x4
MULT = mybir.AluOpType.mult
COPY = mybir.ActivationFunctionType.Copy
IDENTITY = mybir.ActivationFunctionType.Identity

P = 128
SLOTS, TOKENS, D, DV = 1024, 2048, 512, 512
PACK = 4
PASS = P * PACK
BOTH = (0, 1)
BLOCKS = D // P
LAST = BLOCKS - 1
LIST_COLUMNS = PASS // 16
FLOPS = 2 * SLOTS * D * DV

WINDOW_BYTES = TOKENS * 4
HALF_KIB, KIB = 512, 1024
X_WINDOWS = 0
H_WINDOWS = X_WINDOWS + LAST * WINDOW_BYTES
X_CASTS = H_WINDOWS + LAST * WINDOW_BYTES
CAST_PITCH = TOKENS * 2 + 256
TAIL = X_CASTS + LAST * CAST_PITCH


def sbuf_places():
    places = {}
    for k in range(LAST):
        places["x_win%d" % (k + 1)] = places["x_words%d" % k] = X_WINDOWS + k * WINDOW_BYTES
        places["h_win%d" % (k + 1)] = H_WINDOWS + k * WINDOW_BYTES
        places["x_cast%d" % k] = X_CASTS + k * CAST_PITCH
        for s in BOTH:
            places["dz%d%d" % (k, s)] = H_WINDOWS + k * WINDOW_BYTES + s * KIB
            places["factor%d%d" % (k, s)] = X_CASTS + k * CAST_PITCH + 128 + s * 2 * KIB
    places["ts_col"] = X_CASTS
    places["ts_neg"] = X_CASTS + 64
    for s in BOTH:
        places["factor%d%d" % (LAST, s)] = places["x_win%d" % LAST] + (s + 1) * 2 * KIB
    places["dz%d1" % LAST] = TAIL + HALF_KIB
    places["x_codes%d" % (LAST - 1)] = TAIL
    places["x_codes%d" % LAST] = TAIL + KIB
    return places


def psum_banks():
    banks = {}
    for s in BOTH:
        banks["ts_turned%d" % s] = 2 + s
        for k in range(BLOCKS):
            banks["h_turned%d%d" % (k, s)] = s
            banks["dyh_turned%d%d" % (k, s)] = 2 + s
    for k in range(LAST):
        banks["x_turned%d0" % k] = 0
    banks["h_turned%d0" % LAST] = 7
    banks["x_turned%d0" % LAST] = 4
    banks["x_turned%d1" % LAST] = 0
    for j, number in enumerate((5, 6, 1, 7)):
        banks["acc%d" % j] = number
    return banks


def tile_attend_gex_sig_w_kernel(tc, xT, dyT, hT, ts, offs, out):
    nc = tc.nc
    places, banks = sbuf_places(), psum_banks()
    tiles = {}

    with ExitStack() as ctx:
        keep = ctx.enter_context(tc.tile_pool(name="keep", bufs=1))
        psum = ctx.enter_context(tc.psum_pool(name="psum", bufs=1))
        shared = ctx.enter_context(tc.tile_pool(name="shared", bufs=1))

        def sbuf(name, shape, dtype):
            if name not in tiles:
                if name in places:
                    tiles[name] = shared.tile(shape, dtype, name=name, offset=places[name], align_bytes=64)
                else:
                    tiles[name] = keep.tile(shape, dtype, name=name, align_bytes=64)
            return tiles[name]

        def in_psum(name, shape):
            if name not in tiles:
                tiles[name] = psum.tile(shape, F32, name=name, offset=2 * KIB * banks[name])
            return tiles[name]

        def slots(passes):
            return slice(passes[0] * PASS, (passes[-1] + 1) * PASS)

        def block(k):
            return slice(k * P, (k + 1) * P)

        offsets = keep.tile([P, SLOTS // 16], U16, name="offsets")

        def listed(window, passes):
            return window[:].indirect(offsets[:, passes[0] * LIST_COLUMNS : (passes[-1] + 1) * LIST_COLUMNS])

        ts_win = keep.tile([P, TOKENS], F32, name="ts_win")
        nc.vector.memset(ts_win[:], 0.0)

        def load(name, source, k):
            nc.sync.dma_start(sbuf("%s_win%d" % (name, k), [P, TOKENS], F32)[:], source[block(k), :])

        load("x", xT, 0)
        nc.sync.dma_start(offsets[:], offs)
        nc.sync.dma_start(ts_win[0:1, :], ts[0:1, :])
        load("h", hT, 0)
        load("dy", dyT, 0)
        for k in range(1, BLOCKS):
            load("h", hT, k)
            load("x", xT, k)
            load("dy", dyT, k)

        ident = keep.tile([P, P], F32, name="ident")
        make_identity(nc, ident[:])

        dz_codes = [sbuf("dz_codes%d" % s, [P, DV], U32) for s in BOTH]
        dz_scales = [sbuf("dz_scales%d" % s, [P, DV], U8) for s in BOTH]

        def turn(name, gathered, s):
            turned = in_psum(name, [P, PACK, P])
            for t in range(PACK):
                nc.tensor.transpose(turned[:, t, :], gathered[:, s * PASS + t : (s + 1) * PASS : PACK], ident[:])

        def gather_ts():
            ts_row = sbuf("ts_row", [P, SLOTS], F32)
            nc.vector.tensor_copy(ts_row[:], listed(ts_win, BOTH))
            for s in BOTH:
                turn("ts_turned%d" % s, ts_row, s)

        def copy_ts_columns():
            for s in BOTH:
                column = tiles["ts_turned%d" % s][:, :, 0]
                of_pass = slice(PACK * s, PACK * (s + 1))
                nc.scalar.copy(sbuf("ts_col", [P, 2 * PACK], F32)[:, of_pass], column)
                nc.scalar.activation(sbuf("ts_neg", [P, 2 * PACK], F32)[:, of_pass], column, COPY, scale=-1.0)

        def gather_h(k):
            nc.vector.tensor_copy(sbuf("h%d" % k, [P, SLOTS], F32)[:], listed(tiles["h_win%d" % k], BOTH))

        def turn_h(k):
            for s in BOTH:
                turn("h_turned%d%d" % (k, s), tiles["h%d" % k], s)

        def form_factor(k, s):
            factor = sbuf("factor%d%d" % (k, s), [P, PACK, P], F32)
            for t in range(PACK):
                own = slice(PACK * s + t, PACK * s + t + 1)
                nc.scalar.activation(
                    factor[:, t, :],
                    tiles["h_turned%d%d" % (k, s)][:, t, :],
                    IDENTITY,
                    bias=tiles["ts_col"][:, own],
                    scale=tiles["ts_neg"][:, own],
                )

        def gather_dyh(k, passes):
            dyh = sbuf("dyh%d" % k, [P, SLOTS], F32)
            nc.vector.tensor_tensor(
                dyh[:, slots(passes)], listed(tiles["dy_win%d" % k], passes), tiles["h%d" % k][:, slots(passes)], MULT
            )
            for s in passes:
                turn("dyh_turned%d%d" % (k, s), dyh, s)

        def form_dz(k, s):
            nc.vector.tensor_tensor(
                sbuf("dz%d%d" % (k, s), [P, PASS], BF16)[:].rearrange("p (c i t) -> p c t i", i=4, t=PACK),
                tiles["dyh_turned%d%d" % (k, s)][:].rearrange("p t (c i) -> p c t i", i=4),
                tiles["factor%d%d" % (k, s)][:].rearrange("p t (c i) -> p c t i", i=4),
                MULT,
            )

        def quantise_dz(k, s):
            nc.vector.quantize_mx(
                out=dz_codes[s][:, block(k)].bitcast(E5M2X4),
                scales=dz_scales[s][:, block(k)],
                in_=tiles["dz%d%d" % (k, s)][:],
            )

        def cast_x(k):
            nc.scalar.activation(sbuf("x_cast%d" % k, [P, TOKENS], BF16)[:], tiles["x_win%d" % k][:], COPY)

        def gather_x(k, passes):
            pairs = sbuf("x_pairs%d%d" % (k, passes[0]), [P, len(passes) * PASS], BF16)
            nc.scalar.activation(
                pairs[:].rearrange("p (u g e) -> p g u e", u=2, e=2), listed(tiles["x_cast%d" % k], passes), COPY
            )

        def turn_x(k, passes):
            words = tiles["x_pairs%d%d" % (k, passes[0])][:].bitcast(F32)
            turned = in_psum("x_turned%d%d" % (k, passes[0]), [P, PACK, P])
            for q in range(len(passes)):
                for u in range(2):
                    first = (u * len(passes) + q) * P
                    nc.tensor.transpose(turned[:, 2 * q + u, :], words[:, first : first + P], ident[:])

        def copy_x_words(k, passes):
            x_words = sbuf("x_words%d" % k, [P, SLOTS], BF16)
            turned = tiles["x_turned%d%d" % (k, passes[0])][:, 0 : 2 * len(passes), :]
            nc.scalar.copy(
                x_words[:, slots(passes)].bitcast(F32).rearrange("p (q d u) -> p q d u", d=P, u=2),
                turned.rearrange("p (q u) d -> p q d u", u=2),
            )

        def quantise_x(k):
            nc.vector.quantize_mx(
                out=sbuf("x_codes%d" % k, [P, 2 * P], U32)[:].bitcast(E4M3X4),
                scales=sbuf("x_scales%d" % k, [P, 2 * P], U8)[:],
                in_=tiles["x_words%d" % k][:],
            )

        def multiply_and_store(j):
            acc = in_psum("acc%d" % j, [P, DV])
            for s in BOTH:
                nc.tensor.matmul_mx(
                    out=acc[:],
                    lhsT=tiles["x_codes%d" % j][:, block(s)].bitcast(E4M3X4),
                    lhsT_scale=tiles["x_scales%d" % j][:, block(s)],
                    rhs=dz_codes[s][:].bitcast(E5M2X4),
                    rhs_scale=dz_scales[s][:],
                    start=(s == BOTH[0]),
                    stop=(s == BOTH[-1]),
                )
            result = sbuf("result%d" % j, [P, DV], F32)
            if j % 2 == 0:
                nc.scalar.copy(result[:], acc[:])
            else:
                nc.vector.tensor_copy(result[:], acc[:])
            nc.sync.dma_start(out[0, block(j), :], result[:])

        cast_x(0)
        gather_x(0, BOTH)
        gather_ts()
        gather_h(0)
        turn_h(0)
        copy_ts_columns()
        for s in BOTH:
            form_factor(0, s)

        for k in range(LAST):
            gather_dyh(k, BOTH)
            turn_x(k, BOTH)
            gather_h(k + 1)
            cast_x(k + 1)
            copy_x_words(k, BOTH)
            turn_h(k + 1)
            for s in BOTH:
                form_dz(k, s)
            for s in BOTH:
                quantise_dz(k, s)
            if k + 1 < LAST:
                gather_x(k + 1, BOTH)
                for s in BOTH:
                    form_factor(k + 1, s)
                quantise_x(k)

        for s in BOTH:
            form_factor(LAST, s)
            gather_x(LAST, (s,))
        for s in BOTH:
            gather_dyh(LAST, (s,))
        for s in BOTH:
            turn_x(LAST, (s,))
        for s in BOTH:
            copy_x_words(LAST, (s,))
        for s in BOTH:
            form_dz(LAST, s)
            quantise_dz(LAST, s)
        quantise_x(LAST - 1)
        quantise_x(LAST)
        for j in range(BLOCKS):
            multiply_and_store(j)
